import numpy as np, ml_dtypes
CORES = [2,6,10,14,18,22,26,30]
N = 8
import mx_ref
BF = ml_dtypes.bfloat16
def gentries(a):
    return np.ascontiguousarray(a.reshape(8, 16, -1).transpose(0, 2, 1)).reshape(8, -1)
def gtable(e):
    e = np.asarray(e); return np.ascontiguousarray(e.reshape(8, -1, 16).transpose(0, 2, 1)).reshape(128, -1).astype(np.int32)
def gcols(t, e):
    v = np.concatenate([t.reshape(8, 16, -1, 4), np.zeros((8, 16, 1, 4), BF)], axis=2)
    return np.ascontiguousarray(np.stack([v[g][:, e[g]] for g in range(8)])).reshape(128, -1)
def tile(rs):
    return np.stack(rs, axis=2).reshape(128, -1).astype(BF)
def pick(q, e):
    c = np.concatenate([q[0].reshape(128, -1, 4), np.zeros((128, 1, 4), np.uint8)], axis=1); s = np.concatenate([q[1], np.ones((16, 1), np.uint8)], axis=1)
    return (np.ascontiguousarray(c[:, e].reshape(128, -1)), np.ascontiguousarray(s[:, e]))
def join(*qs):
    return (np.concatenate([q[0] for q in qs], axis=1), np.concatenate([q[1] for q in qs], axis=1))
def put(q, e, v):
    c, s = q[0].reshape(128, -1, 4).copy(), q[1].copy(); c[:, e] = v[0].reshape(128, -1, 4); s[:, e] = v[1]
    return (c.reshape(128, -1), s)
def pk(c, s):
    return (np.ascontiguousarray(c), mx_ref.live(s))
def emit(q):
    return q[0], q[1]
def packed(v, rng):
    q = [mx_ref.quantize(np.ascontiguousarray(v[r])) for r in range(N)]
    return np.stack([a for a, b in q]), np.stack([mx_ref.plane(b, rng) for a, b in q])
def values_of_codes():
    e, c = np.zeros((128, 128, 4), np.float32), np.zeros((128, 2, 4), np.uint8)
    e[np.arange(128), np.arange(128), 0] = 1
    c[:127, :, 0] = np.arange(256).reshape(2, 128).T[:127]
    return mx_ref.matmul(mx_ref.quantize(e.reshape(128, 512).astype(BF)), (c.reshape(128, 8), np.full((16, 2), 127, np.uint8))).T.reshape(-1).astype(np.float64)
CODE_VALUE, SCALE_VALUE = values_of_codes(), 2.0 ** (np.arange(256) - 127.0)
def decode(q):
    return (CODE_VALUE[q[0]].reshape(16, 8, -1, 4) * SCALE_VALUE[q[1]][:, None, :, None] + 0.0).reshape(128, -1).astype(np.float32)
def f(rng, *shape):
    return mx_ref.flush((rng.standard_normal(shape, dtype=np.float32) * np.exp2(rng.integers(-2, 3, shape[:-1] + (1,)))).astype(BF))
def wide(rng, *shape, cols=0):
    v = rng.standard_normal(shape, dtype=np.float32) * np.exp2(rng.integers(-12, 13, shape)).astype(np.float32)
    if cols: v *= np.repeat(np.exp2(rng.integers(-cols, cols + 1, shape[:-2] + (1, shape[-1] // 4))) * (rng.random(shape[:-2] + (1, shape[-1] // 4)) > 0.0625), 4, axis=-1).astype(np.float32)
    return mx_ref.flush(v.astype(BF))
C = 384
STEP = [1, 2, 4]
def big(v):
    v = v.astype(np.float32)
    v[np.abs(v) < np.float32(2.0 ** -16)] = 0
    return v.astype(BF)
def numbers_of(rng):
    return {"x": big(f(rng, N, 128, 4 * C)), "u": np.array(f(rng, N, 128, 512)), "v": np.array(f(rng, N, 128, 512))}
def stored(k, t):
    return {"gl": np.stack([gtable(k[r]) for r in range(N)]), "ht": np.stack([gtable(t[r]) for r in range(N)])}
def lists(rng):
    e = np.tile(np.arange(C), (N, 8, 1))
    k = np.stack([rng.permuted(e, axis=2), rng.permuted(e, axis=2)], axis=3).reshape(N, 8, 2 * C)
    return stored(k, rng.integers(0, C, (N, 8, C)))
def layers(rng):
    return big(f(rng, N, 128, 2048)).reshape(N, 8, 16, 4, 8, 16, 4)
def weights(rng, w):
    c, p = packed(np.ascontiguousarray(w).reshape(N, 128, 2048), rng)
    return {"wc": c, "ws": p}
def setup_inputs(rng):
    return {**numbers_of(rng), **lists(rng), **weights(rng, layers(rng))}
def setup_inputs_ties(rng):
    d = numbers_of(rng)
    o = rng.permutation(N)
    k = rng.integers(-1, 2, (N, 8, C)).astype(np.float32)
    k[o[1]] = 1
    x = d["x"].reshape(N, 8, 16, C, 4)
    x[:, :, 0] = 0
    x[:, :, 0, :, 0] = k.astype(BF)
    c = np.ones(N, np.float32)
    c[o[0]] = 0
    c[o[2]] = -1
    u = d["u"].reshape(N, 128, 128, 4)
    u[:, :, ::16] = 0
    for h in range(0, 128, 16): u[:, h, h, 0] = c.astype(BF)
    w = layers(rng)
    w[:, :, :, :, :, :8] = 0
    return {"x": x.reshape(N, 128, 4 * C), "u": u.reshape(N, 128, 512), "v": d["v"], **lists(rng), **weights(rng, w)}
def setup_inputs_near(rng):
    d = numbers_of(rng)
    o = rng.permutation(N) % 2
    k = np.where(o == 0, 2.0 ** -30, 1.0).astype(np.float32)
    x = np.zeros((N, 8, 16, C, 4), np.float32)
    s = rng.integers(-1, 2, (N, 8, C)) * k[:, None, None]
    x[:, :, 0, :, 0] = 1.125 * s
    x[:, :, 1, :, 0] = -1.25 * s
    for r in range(N):
        for g in rng.permutation(8)[:4]: x[r, g, 0, rng.integers(C), 0] = 2.0 ** 30 * rng.choice([-1.0, 1.0])
    i = np.arange(N)
    e = ((i ^ (i >> 1) ^ (i >> 2))[:, None] + rng.permutation(8)) % 2
    a = (1 + (2 * rng.integers(0, 64, (N, 8, 8, C, 4)) + 1) * 2.0 ** -7) * np.exp2(12.0 - rng.integers(8, 15, (N, 8, 8, C, 4)))
    a[:, :, 0, :, 0] = -1.96875 * 2.0 ** 12
    a = np.where(e[:, :, None, None, None] == 0, -2.0 ** 26, a)
    x[:, :, 8:] = np.where(rng.random((N, 8, 1, C, 1)) < 0.5, a, 0.0)
    u = d["u"].reshape(N, 128, 128, 4)
    u[:, :, ::16] = 0
    for h in range(0, 128, 16):
        u[:, h, h, 0] = (1.125 * k).astype(BF)
        u[:, h + 1, h, 0] = k.astype(BF)
    w = layers(rng)
    w[:, :, :8] = 0
    w[:, :, :, :, :, :8] = 0
    return {"x": x.reshape(N, 128, 4 * C).astype(BF), "u": u.reshape(N, 128, 512), "v": d["v"], **lists(rng), **weights(rng, w)}
def setup_inputs_late(rng):
    d = numbers_of(rng)
    c = (rng.permutation(N) % 2 * 2.0 - 1.0).astype(np.float32).astype(BF)
    x = d["x"].reshape(N, 8, 16, C, 4)
    x[:, :, 0] = c[:, None, None, None]
    u = d["u"].reshape(N, 128, 128, 4)
    u[:, :, ::16] = 0
    for h in range(0, 128, 16): u[:, h, h, 0] = 1
    w = layers(rng)
    w[:, :, :, :, :, 0] = (w[:, :, :, :, :, 0].astype(np.float32) * 4).astype(BF)
    return {"x": x.reshape(N, 128, 4 * C), "u": u.reshape(N, 128, 512), "v": d["v"], **lists(rng), **weights(rng, w)}
def setup_inputs_ends(rng):
    d = numbers_of(rng)
    o, e = rng.permutation(N) % 4, rng.permutation(N) % 4
    s = rng.choice([-1.0, 1.0], (N, 128, C, 4))
    s[o == 0] = -1
    s[o == 1] = rng.choice([-1.0, 1.0], (N, 1, C, 1))[o == 1]
    x = s * (0.955 + 0.02 * rng.random((N, 128, C, 4))) * 2.0 ** 30
    x[:, :8] = 0
    x[:, 13] = -240 * 2.0 ** 22
    x[:, 14] = -249 * 2.0 ** 22
    x[:, 15] = 0
    x[o == 3] = 2.0 ** -30
    size = np.where(o == 3, 2.0 ** -30, 2.0 ** 30)
    a = np.stack([rng.permutation(8) % 2 * 2.0 - 1.0 for r in range(N)]) * size[:, None]
    u = d["u"].reshape(N, 128, 128, 4)
    u[:, :, ::16] = a.astype(np.float32).astype(BF)[:, None, :, None]
    v = rng.choice([-1.0, 1.0], (N, 128, 512)) * size[:, None, None]
    t = rng.integers(0, C, (N, 8, C))
    t[o == 0] = C - 1
    t[o == 1] = 0
    t[o == 2] = rng.integers(0, 2, (8, C)) * (C - 1)
    k = rng.integers(0, C, (N, 8, 2 * C))
    k[e == 0] = C - 1
    k[e == 1] = 0
    k[e == 1, 7] = C - 1
    k[e == 2] = np.arange(2 * C) % 2 * (C - 1)
    w = np.zeros((N, 128, 4, 128, 4), np.float32)
    i = np.arange(128)
    for b in range(4):
        w[:, i, b, i, b] = np.where(o == 3, 16.0, -0.25)[:, None]
        for r in range(N):
            if o[r] < 3:
                w[r, :8, b, :8, b] = 64 * np.eye(8)
                w[r, 13:16, b, 13:16, b] = [[0, 0, -64], [0, 0, 64], [0, 0, 0]]
    return {"x": x.astype(np.float32).reshape(N, 128, 4 * C).astype(BF), "u": u.reshape(N, 128, 512), "v": v.astype(np.float32).astype(BF), **stored(k, t), **weights(rng, w.astype(BF))}
def setup_inputs_spread(rng):
    d = setup_inputs(rng)
    d["x"] = big(wide(rng, N, 128, 4 * C, cols=6))
    return d
def check_inputs(d):
    b = []
    for k in ("x", "u", "v"):
        a = np.abs(d[k].astype(np.float32))
        if not (np.isfinite(a).all() and ((a == 0) | (a >= 2.0 ** -30) & (a <= 2.0 ** 30)).all()): b.append("a value of " + k)
    for k in ("gl", "ht"):
        if not ((d[k] >= 0) & (d[k] < C)).all(): b.append("an entry of " + k)
    none, least, most = [emit(mx_ref.quantize(np.full((128, 16), k, np.float32).astype(BF)))[1][0, 0] for k in (0.0, 2.0 ** -30, 2.0 ** 30)]
    for r in range(N):
        if ((d["wc"][r] == 0x7F) | (d["wc"][r] == 0xFF)).any(): b.append("wc: a code that is no number")
        s = mx_ref.live(d["ws"][r])
        if ((s != none) & ((s < least) | (s > most))).any(): b.append("ws: a scale out of range")
        if (((d["wc"][r].reshape(16, 8, 512, 4) & 0x7F) != 0) & (s == none)[:, None, :, None]).any(): b.append("wc: a code other than zero under the scale of zeros")
    return b
def reference(x, u, v, gl, ht, wc, ws):
    qu = [mx_ref.quantize(u[r]) for r in range(N)]
    lay = [pk(wc[r], ws[r]) for r in range(N)]
    guest, host = [gentries(gl[r]) for r in range(N)], [gentries(ht[r]) for r in range(N)]
    now = [x[r] for r in range(N)]
    y, pl = np.zeros((N, 128, C), np.float32), np.zeros((N, 8, C), np.float32)
    for step in STEP:
        q = [mx_ref.quantize(now[r]) for r in range(N)]
        bit = [(mx_ref.matmul(qu[r], q[r])[::16] > 0).astype(np.int64) for r in range(N)]
        made = []
        for r in range(N):
            p = r ^ step
            at, there = np.zeros((9, C), np.int64), np.zeros((8, C), np.int64)
            at[0] = np.arange(C)
            for g in range(8):
                there[g] = host[p][g][at[g]]
                at[g + 1] = guest[r][g][2 * at[g] + bit[p][g][there[g]]]
            far = gcols(decode(q[p]).astype(BF), there)
            z = mx_ref.quantize(np.maximum(gcols(now[r], at[:8]).astype(np.float32), far.astype(np.float32)).astype(BF))
            made.append(tile([mx_ref.matmul(pick(lay[r], np.arange(128 * b, 128 * b + 128)), z) * np.float32(0.015625) + now[r][:, b::4].astype(np.float32) for b in range(4)]))
            pl[r] = at[1:]
        now = made
    oc, osc = np.zeros((N, 128, 4 * C), np.uint8), np.zeros((N, 16, C), np.uint8)
    for r in range(N):
        q = mx_ref.quantize(now[r])
        y[r] = mx_ref.matmul(mx_ref.quantize(v[r]), q)
        oc[r], osc[r] = emit(q)
    return {"y": y, "pl": pl, "oc": oc, "osc": osc}

import numpy as np
from concourse.mybir import dt, AluOpType, ActivationFunctionType

C = 384
H = 192
NH = 2
STEP = [1, 2, 4]
ALU = AluOpType
COPY = ActivationFunctionType.Copy

SCRATCH = {
    "ut": ("sbuf", [128, 512], "bfloat16"), "vt": ("sbuf", [128, 512], "bfloat16"),
    "uq": ("sbuf", [128, 128], "float8_e4m3fn_x4"), "us": ("sbuf", [128, 128], "uint8"),
    "uqr": ("sbuf", [128, 128], "float8_e4m3fn_x4"), "usr": ("sbuf", [128, 128], "uint8"),
    "vq": ("sbuf", [128, 128], "float8_e4m3fn_x4"), "vs": ("sbuf", [128, 128], "uint8"),
    "wq": ("sbuf", [128, 512], "float8_e4m3fn_x4"), "wsp": ("sbuf", [128, 512], "uint8"),
    "e0": ("sbuf", [128, 2048], "bfloat16"), "et": ("sbuf", [128, 2048], "bfloat16"),
    "eq": ("sbuf", [128, 512], "float8_e4m3fn_x4"), "es": ("sbuf", [128, 512], "uint8"),
    "x64": ("sbuf", [128, 4 * C], "bfloat16"), "lx": ("sbuf", [128, 4 * C], "bfloat16"),
    "m": ("sbuf", [128, 4 * C], "bfloat16"), "z": ("sbuf", [128, 4 * C], "bfloat16"),
    "zq": ("sbuf", [128, C], "float8_e4m3fn_x4"), "zs": ("sbuf", [128, C], "uint8"),
    "xq": ("sbuf", [128, C], "float8_e4m3fn_x4"), "xs": ("sbuf", [128, C], "uint8"),
    "uu": ("sbuf", [128, 8 * H], "float32"),
    "gli": ("sbuf", [128, 48], "int32"), "gl16": ("sbuf", [128, 48], "uint16"),
    "hti": ("sbuf", [128, 24], "int32"), "ht16": ("sbuf", [128, 24], "uint16"), "ht4": ("sbuf", [128, 96], "uint16"),
    "glf": ("sbuf", [128, 768], "float32"),
    "bits": ("sbuf", [128, C], "bfloat16"), "t1": ("sbuf", [128, C], "float32"),
    "ft": ("sbuf", [128, 8 * C], "bfloat16"),
    "w1": ("sbuf", [128, 48], "float32"), "w2": ("sbuf", [128, 48], "float32"),
    "ov0": ("sbuf", [128, 4], "uint16"), "ov": ("sbuf", [128, 4], "uint16"), "vo": ("sbuf", [128, 32], "uint16"),
    "ident": ("sbuf", [128, 768], "float32"), "ip": ("sbuf", [128, 1], "int32"), "k8": ("sbuf", [128, 8], "int32"),
    "row": ("sbuf", [128, 48], "float32"), "c16": ("sbuf", [128, 24], "float32"), "upi": ("sbuf", [128, 8], "int32"),
    "up": ("sbuf", [128, 8], "uint16"), "ia": ("sbuf", [128, 4], "int32"), "fa": ("sbuf", [128, 4], "float32"),
    "kk": ("sbuf", [128, 8], "int32"), "kf": ("sbuf", [128, 8], "float32"), "jl": ("sbuf", [128, 24], "uint16"),
    "jw": ("sbuf", [128, 4], "float32"), "mask": ("sbuf", [128, 48], "float32"), "keep": ("sbuf", [128, 48], "float32"),
    "ysb": ("sbuf", [128, C], "float32"), "plb": ("sbuf", [128, C], "float32"), "plc": ("sbuf", [128, C], "float32"),
    "vl8": ("dram", [128, 24], "uint16"), "vland8": ("sbuf", [128, 24], "uint16"),
    "psa": ("psum", [128, 2048], "float32"), "psb": ("psum", [128, 2048], "float32"),
}
for _r in range(3):
    SCRATCH["lq%d" % _r] = ("sbuf", [128, C], "float8_e4m3fn_x4")
    SCRATCH["ls%d" % _r] = ("sbuf", [128, C], "uint8")
    SCRATCH["landq%d" % _r] = ("sbuf", [128, C], "float8_e4m3fn_x4")
    SCRATCH["lands%d" % _r] = ("sbuf", [128, C], "uint8")
    SCRATCH["glr%d" % _r] = ("sbuf", [128, 48], "uint16")
    SCRATCH["ge%d" % _r] = ("sbuf", [128, C], "float32")
    SCRATCH["gd%d" % _r] = ("sbuf", [128, C], "float32")
    SCRATCH["vl%d" % _r] = ("dram", [128, 24], "uint16")
    SCRATCH["vland%d" % _r] = ("sbuf", [128, 24], "uint16")
for _r in range(4):
    SCRATCH["x_%d" % _r] = ("sbuf", [128, 4 * C], "bfloat16")

SEMAPHORES = ["cv", "cs", "ct", "cg", "sent", "arrl8",
              "ld_gl", "ld_ht", "ld_u", "ld_w", "ld_v", "ld_x0", "ld_x1", "pre", "v8",
              "st0", "st1", "stp", "stq"]
for _r in range(3):
    SEMAPHORES += ["arrq%d" % _r, "arrl%d" % _r, "arrg%d" % _r, "fb%d" % _r, "vla%d" % _r, "vlb%d" % _r]


def tracker(g, T):
    queue = {"v": g.vector, "s": g.scalar, "t": g.tensor, "g": g, "y": g.sync}
    csem = {"v": "cv", "s": "cs", "t": "ct", "g": "cg"}
    count = {k: 0 for k in csem}
    know = {k: {} for k in queue}
    clock, writer, readers = {}, {}, {}
    total, waited = {}, {}

    def merge(a, b):
        for s, n in b.items():
            if a.get(s, 0) < n:
                a[s] = n

    def need(e, toks):
        todo = {}
        for s, n in toks:
            if know[e].get(s, 0) < n:
                todo[s] = max(todo.get(s, 0), n)
        for s in list(todo):
            for s2 in list(todo):
                if s2 != s and s in todo and clock.get((s2, todo[s2]), {}).get(s, 0) >= todo[s]:
                    del todo[s]
        for s, n in todo.items():
            queue[e].wait_ge(T.sem[s], n)
            waited[s] = max(waited.get(s, 0), n)
            merge(know[e], clock.get((s, n), {}))
            merge(know[e], {s: n})

    def deps(e, reads, writes):
        own = csem.get(e)
        toks = [writer[k] for k in list(reads) + list(writes) if k in writer]
        for k in writes:
            toks += [t for t in readers.get(k, []) if t[0] != own]
        return toks

    def record(tok, reads, writes):
        for k in reads:
            readers.setdefault(k, []).append(tok)
        for k in writes:
            writer[k] = tok
            readers[k] = []

    def op(e, fn, reads, writes):
        need(e, deps(e, reads, writes))
        count[e] += 1
        tok = (csem[e], count[e])
        fn(queue[e]).then_inc(T.sem[csem[e]], 1)
        total[csem[e]] = count[e]
        clock[tok] = dict(know[e])
        clock[tok][tok[0]] = tok[1]
        record(tok, reads, writes)

    def dma(e, sem, n, out, in_, reads, writes):
        d = deps(e, reads, writes)
        need(e, [t for t in d if t[0] != sem])
        tok = (sem, 16 * n)
        queue[e].dma_start(out, in_).then_inc(T.sem[sem], 16)
        total[sem] = 16 * n
        c = clock.setdefault(tok, dict(know[e]))
        for s in list(c):
            c[s] = max(c[s], know[e].get(s, 0))
        record(tok, reads, writes)

    def arrives(sem, n, keys):
        total[sem] = n
        for k in keys:
            writer[k] = (sem, n)

    def before(e, reads):
        need(e, [writer[k] for k in reads])

    def finish():
        for s, n in total.items():
            if waited.get(s, 0) < n:
                g.wait_ge(T.sem[s], n)
    return op, dma, arrives, before, finish, total


def rank_program(g, core, T, topo):
    rank = T.rank_of(core)
    if rank is None:
        return
    op, dma, arrives, before, finish, total = tracker(g, T)
    partner = [T.cores[rank ^ s] for s in STEP]

    def send(dst, out, in_, sem):
        e = topo.engines(core, dst)[:8]
        rid, pid = topo.addr(dst)[:2]
        g.remote_dma(out, in_, T.sem[sem], T.sem.sent, pid, rid, sum(1 << k for k in e))
        total["sent"] = total.get("sent", 0) + len(e)
        return len(e)

    ne = [len(topo.engines(core, p)[:8]) for p in partner]
    for r in range(3):
        arrives("arrq%d" % r, 2 * ne[r], ["landq%d" % r])
        arrives("arrl%d" % r, ne[r], ["vland%d" % r])
        arrives("arrg%d" % r, ne[r], ["glr%d" % r])
    arrives("arrl8", ne[2], ["vland8"])

    def half(name, h):
        return ["%s.%d.%d" % (name, b, h) for b in range(4)]

    def whole(name):
        return half(name, 0) + half(name, 1)

    dma("y", "ld_gl", 1, T.gli[:], T.gl[:], [], ["gli"])
    dma("s", "ld_u", 1, T.ut[:], T.u[:], [], ["ut"])
    dma("y", "ld_x0", 1, T.x_0[:, 0:4 * H], T.x[:, 0:4 * H], [], half("x_0", 0))
    dma("s", "ld_x1", 1, T.x_0[:, 4 * H:], T.x[:, 4 * H:], [], half("x_0", 1))
    dma("y", "ld_ht", 1, T.hti[:], T.ht[:], [], ["hti"])
    dma("y", "ld_w", 2, T.wq[:].bitcast(dt.uint8), T.wc[:], [], ["wq"])
    dma("y", "ld_w", 2, T.wsp[:], T.ws[:], [], ["wsp"])
    dma("y", "ld_v", 1, T.vt[:], T.v[:], [], ["vt"])

    op("g", lambda q: q.iota(T.upi[:], [[16, 8]], 0, 0), [], ["upi"])
    op("g", lambda q: q.iota(T.ip[:], [[0, 1]], 0, 1), [], ["ip"])
    op("g", lambda q: q.iota(T.k8[:], [[-16, 8]], 128, 1), [], ["k8"])
    op("g", lambda q: q.iota(T.row[:], [[0, 3], [1, 16]], 0, 0, allow_small_or_imprecise_dtypes=True), [], ["row"])
    op("g", lambda q: q.iota(T.c16[:], [[16, 24]], 0, 0, allow_small_or_imprecise_dtypes=True), [], ["c16"])
    op("g", lambda q: q.iota(T.ident[:], [[1, 768]], 0, 0, allow_small_or_imprecise_dtypes=True), [], ["ident"])
    V = lambda fn, r, w: op("v", fn, r, w)
    S = lambda fn, r, w: op("s", fn, r, w)
    V(lambda q: q.memset(T.e0[:], 1.0), [], ["e0"])
    V(lambda q: q.tensor_copy(T.up[:], T.upi[:]), ["upi"], ["up"])
    V(lambda q: q.tensor_scalar(T.ia[:, 0:1], T.ip[:], 15, None, ALU.bitwise_and), ["ip"], ["ia0"])
    V(lambda q: q.tensor_scalar(T.ia[:, 1:2], T.ip[:], 7, None, ALU.bitwise_and), ["ip"], ["ia1"])
    V(lambda q: q.tensor_scalar(T.ia[:, 2:3], T.ip[:], 3, None, ALU.arith_shift_right), ["ip"], ["ia2"])
    V(lambda q: q.tensor_scalar(T.kk[:], T.k8[:], 4, 7, ALU.arith_shift_right, ALU.bitwise_and), ["k8"], ["kk"])
    V(lambda q: q.tensor_copy(T.fa[:, 0:1], T.ia[:, 0:1]), ["ia0"], ["fa0"])
    V(lambda q: q.tensor_scalar(T.fa[:, 1:2], T.ia[:, 1:2], 48.0, None, ALU.mult), ["ia1"], ["fa1"])
    V(lambda q: q.tensor_copy(T.fa[:, 2:3], T.ia[:, 2:3]), ["ia2"], ["fa2"])
    V(lambda q: q.tensor_scalar(T.kf[:], T.kk[:], 384.0, 192.0, ALU.mult, ALU.add), ["kk"], ["kf"])
    V(lambda q: q.tensor_scalar(T.keep[:], T.row[:], 0.0, None, ALU.not_equal), ["row"], ["keep"])
    V(lambda q: q.tensor_scalar(T.mask[:], T.row[:], T.fa[:, 0:1], None, ALU.is_equal), ["row", "fa0"], ["mask"])
    V(lambda q: q.tensor_scalar(T.jl[:], T.c16[:], T.fa[:, 0:1], None, ALU.add), ["c16", "fa0"], ["jl"])
    V(lambda q: q.tensor_scalar(T.jw[:, 0:3], T.c16[:, 0:3], T.fa[:, 1:2], T.fa[:, 2:3], ALU.add, ALU.add),
      ["c16", "fa1", "fa2"], ["jw"])
    V(lambda q: q.tensor_scalar(T.ov0[:, 0:3], T.jw[:, 0:3], T.kf[:, 0:1], -192.0, ALU.add, ALU.add), ["jw", "kf"], ["ov0"])
    V(lambda q: q.tensor_copy(T.gl16[:], T.gli[:]), ["gli"], ["gl16"])

    def send_table(r):
        before("g", ["gl16"])
        send(partner[r], T["glr%d" % r][:], T.gl16[:], "arrg%d" % r)
    send_table(0)
    op("g", lambda q: q.affine_select(T.et[:], T.e0[:], [[-1, 4], [8, 128], [1, 4]], ALU.is_equal, 0.0, 0, -8), ["e0"], ["et"])
    send_table(1)
    send_table(2)

    V(lambda q: q.quantize_mx(T.uq[:], T.us[:], T.ut[:]), ["ut"], ["uq"])
    V(lambda q: q.tensor_copy(T.uqr[:].bitcast(dt.uint32), T.uq[:].bitcast(dt.uint32).indirect(T.up[:])), ["uq", "up"], ["uqr"])
    V(lambda q: q.tensor_copy(T.usr[:], T.us[:].indirect(T.up[:])), ["uq", "up"], ["usr"])
    V(lambda q: q.tensor_copy(T.ht16[:], T.hti[:]), ["hti"], ["ht16"])
    for t in range(4):
        V(lambda q, t=t: q.tensor_scalar(T.ht4[:, 24 * t:24 * t + 24], T.hti[:], 4.0, float(t), ALU.mult, ALU.add),
          ["hti"], ["ht4.%d" % t])
    for k in range(3):
        dma("y", "pre", 4, T["vl%d" % k][:], T.jl[:], ["jl"], ["vl%d.%d" % (k, b) for b in range(8)])
    dma("y", "pre", 4, T.vl8[:], T.jl[:], ["jl"], ["vl8"])

    def quantise_state(r, h):
        X = T["x_%d" % r]
        V(lambda q: q.quantize_mx(T.xq[:, H * h:H * h + H], T.xs[:, H * h:H * h + H], X[:, 4 * H * h:4 * H * h + 4 * H]),
          half("x_%d" % r, h), ["xq.%d" % h])

    def signs(h):
        op("t", lambda q: q.matmul_mx(T.psb[:, 512 * h:512 * h + H], T.uqr[:], T.usr[:], T.xq[:, H * h:H * h + H],
                                      T.xs[:, H * h:H * h + H], True, True), ["uqr", "usr", "xq.%d" % h], ["psb.%d" % h])
        V(lambda q: q.tensor_scalar(T.bits[:, H * h:H * h + H], T.psb[:, 512 * h:512 * h + H], 0.0, None, ALU.is_gt),
          ["psb.%d" % h], ["bits.%d" % h])

    def lay_table(r):
        S(lambda q: q.activation(T.glf[:], T.ident[:].indirect(T["glr%d" % r][:]), COPY), ["ident", "glr%d" % r], ["glf"])

    def split_table(r):
        V(lambda q: q.tensor_scalar(T["ge%d" % r][:], T.glf[:, 0:768:2], -192.0, None, ALU.add), ["glf"], ["ge%d" % r])
        V(lambda q: q.tensor_tensor(T["gd%d" % r][:], T.glf[:, 1:768:2], T.glf[:, 0:768:2], ALU.subtract), ["glf"], ["gd%d" % r])

    for h in range(NH):
        quantise_state(0, h)
        signs(h)
    lay_table(0)
    split_table(0)

    for r in range(3):
        last = r == 2
        xn, X, Y = "x_%d" % r, T["x_%d" % r], T["x_%d" % (r + 1)]
        lq, ls = T["lq%d" % r], T["ls%d" % r]

        def lay(e, t):
            fn = {"v": lambda q: q.tensor_copy(T.lx[:, t:4 * C:4], X[:].indirect(T.ht4[:, 24 * t:24 * t + 24])),
                  "s": lambda q: q.activation(T.lx[:, t:4 * C:4], X[:].indirect(T.ht4[:, 24 * t:24 * t + 24]), COPY)}[e]
            op(e, fn, whole(xn) + ["ht4.%d" % t], ["lx.%d" % t])
        lay("s", 0)
        lay("s", 1)
        V(lambda q: q.tensor_tensor(T.t1[:], T.bits[:].indirect(T.ht16[:]), T["gd%d" % r][:], ALU.mult),
          ["bits.0", "bits.1", "ht16", "gd%d" % r], ["t1"])
        V(lambda q: q.tensor_tensor(T.ft[:, 0:C], T.t1[:], T["ge%d" % r][:], ALU.add), ["t1", "ge%d" % r], ["ft.0"])
        for k in range(1, 8):
            a, b = 16 * k, C * k
            dma("y", "fb%d" % r, 14, T.ft[a:128, b:b + C], T.ft[0:128 - a, 0:C], ["ft.0"], ["ft.%d.a" % k])
            dma("s", "fb%d" % r, 14, T.ft[0:a, b:b + C], T.ft[128 - a:128, 0:C], ["ft.0"], ["ft.%d.b" % k])
        lay("v", 2)
        lay("v", 3)
        V(lambda q: q.quantize_mx(lq[:], ls[:], T.lx[:]), ["lx.%d" % t for t in range(4)], ["lq%d" % r])
        before("g", ["lq%d" % r])
        send(partner[r], T["landq%d" % r][:].bitcast(dt.uint8), lq[:].bitcast(dt.uint8), "arrq%d" % r)
        send(partner[r], T["lands%d" % r][:], ls[:], "arrq%d" % r)
        S(lambda q: q.activation(T.x64[:], X[:], COPY, scale=64.0), whole(xn), whole("x64"))
        if not last:
            lay_table(r + 1)
        if r == 0:
            V(lambda q: q.quantize_mx(T.eq[:], T.es[:], T.et[:]), ["et"], ["eq"])
            V(lambda q: q.quantize_mx(T.vq[:], T.vs[:], T.vt[:]), ["vt"], ["vq"])
        tables = ["ft.0"] + ["ft.%d.%s" % (k, c) for k in range(1, 8) for c in "ab"]

        def step(s):
            o, ok = (T.ov0, "ov0") if s == 0 else (T.ov, "ov")
            V(lambda q: q.tensor_tensor(T.w1[:], T.ft[:].indirect(o[:, 0:3]), T.mask[:], ALU.mult), tables + [ok, "mask"], ["w1"])
            V(lambda q: q.tensor_tensor_scan(T.w2[:], T.keep[:], T.w1[:], 0.0, ALU.mult, ALU.add), ["keep", "w1"], ["w2"])
            top = 7 if last else 6

            def offsets():
                V(lambda q: q.tensor_scalar(T.ov[:, 0:3], T.w2[:, 15:48:16], T.kf[:, s + 1:s + 2], None, ALU.add),
                  ["w2", "kf"], ["ov"])

            def places():
                V(lambda q: q.tensor_scalar(T.vo[:, 4 * s:4 * s + 3], T.w2[:, 15:48:16], 192.0, None, ALU.add), ["w2"], ["vo.%d" % s])
                if s < 7:
                    sem, n = ("vla%d" % r, 6) if s < 6 else ("vlb%d" % r, 1)
                    dma("y", sem, n, T["vl%d" % r][16 * s + 16:16 * s + 32, :], T.vo[:, 4 * s:4 * s + 3], ["vo.%d" % s],
                        ["vl%d.%d" % (r, s + 1)])
                else:
                    dma("y", "v8", 1, T.vl8[0:16, :], T.vo[:, 28:31], ["vo.7"], ["vl8"])
            if s >= 6:
                places()
                if s < top:
                    offsets()
            else:
                offsets()
                places()
        for s in range(7):
            step(s)
        before("g", ["vl%d.%d" % (r, b) for b in range(8)])
        send(partner[r], T["vland%d" % r][:], T["vl%d" % r][:], "arrl%d" % r)
        if last:
            step(7)
            before("g", ["vl8"])
            send(partner[r], T.vland8[:], T.vl8[:], "arrl8")
        else:
            split_table(r + 1)
        for b in range(4):
            op("t", lambda q, b=b: q.matmul_mx(T.psa[:, 512 * b:512 * b + C], T.eq[:, 128 * b:128 * b + 128], T.es[:, 128 * b:128 * b + 128],
                                               T["landq%d" % r][:], T["lands%d" % r][:], True, True), ["eq", "landq%d" % r], ["psa.%d" % b])
            V(lambda q, b=b: q.tensor_tensor(T.m[:, C * b:C * b + C], T.psa[:, 512 * b:512 * b + C], X[:, b:4 * C:4], ALU.max),
              ["psa.%d" % b] + whole(xn), ["m.%d" % b])
        for h in range(NH):
            off = T["vland%d" % r][:, 12 * h:12 * h + 12]
            for b in range(4):
                e = "v" if b < 2 else "s"
                win, out = T.m[:, C * b:C * b + C].indirect(off), T.z[:, 4 * H * h + b:4 * H * h + 4 * H:4]
                fn = {"v": lambda q: q.tensor_copy(out, win), "s": lambda q: q.activation(out, win, COPY)}[e]
                op(e, fn, ["m.%d" % b, "vland%d" % r], ["z.%d.%d" % (b, h)])
        for h in range(NH):
            V(lambda q: q.quantize_mx(T.zq[:, H * h:H * h + H], T.zs[:, H * h:H * h + H], T.z[:, 4 * H * h:4 * H * h + 4 * H]),
              half("z", h), ["zq.%d" % h])
            ps, pn = (T.psb, "psb") if h == 0 else (T.psa, "psa")
            for b in range(4):
                op("t", lambda q: q.matmul_mx(ps[:, 512 * b:512 * b + H], T.wq[:, 128 * b:128 * b + 128], T.wsp[:, 128 * b:128 * b + 128],
                                              T.zq[:, H * h:H * h + H], T.zs[:, H * h:H * h + H], True, True),
                   ["wq", "wsp", "zq.%d" % h], ["%s.%d" % (pn, b)])
        for h in range(NH):
            ps, pn = (T.psb, "psb") if h == 0 else (T.psa, "psa")
            for b in range(4):
                u = T.uu[:, (4 * h + b) * H:(4 * h + b + 1) * H]
                s0 = slice(4 * H * h + b, 4 * H * h + 4 * H, 4)
                V(lambda q: q.tensor_tensor(u, ps[:, 512 * b:512 * b + H], T.x64[:, s0], ALU.add),
                  ["%s.%d" % (pn, b), "x64.%d.%d" % (b, h)], ["uu.%d.%d" % (b, h)])
                S(lambda q: q.activation(Y[:, s0], u, COPY, scale=0.015625), ["uu.%d.%d" % (b, h)], ["x_%d.%d.%d" % (r + 1, b, h)])
        for h in range(NH):
            quantise_state(r + 1, h)
            if not last:
                signs(h)
    for h in range(NH):
        c0, c1 = H * h, H * h + H
        op("t", lambda q: q.matmul_mx(T.psb[:, 512 * h:512 * h + H], T.vq[:], T.vs[:], T.xq[:, c0:c1], T.xs[:, c0:c1], True, True),
           ["vq", "xq.%d" % h], ["psb.%d" % h])
        sem = "st%d" % h
        dma("y", sem, 6, T.oc[:, 4 * c0:4 * c1], T.xq[:, c0:c1].bitcast(dt.uint8), ["xq.%d" % h], [])
        for k in range(4):
            dma("s" if k % 2 else "y", sem, 6, T.osc[4 * k:4 * k + 4, c0:c1], T.xs[32 * k:32 * k + 4, c0:c1], ["xq.%d" % h], [])
        V(lambda q: q.tensor_copy(T.ysb[:, c0:c1], T.psb[:, 512 * h:512 * h + H]), ["psb.%d" % h], ["ysb.%d" % h])
        dma("y", sem, 6, T.y[:, c0:c1], T.ysb[:, c0:c1], ["ysb.%d" % h], [])
    S(lambda q: q.activation(T.plb[:], T.ident[:, 0:C].indirect(T.vland2[:]), COPY), ["ident", "vland2"], ["plb"])
    dma("s", "stp", 1, T.pl[0:7, :], T.plb[16:128:16, :], ["plb"], [])
    S(lambda q: q.activation(T.plc[:], T.ident[:, 0:C].indirect(T.vland8[:]), COPY), ["ident", "vland8"], ["plc"])
    dma("s", "stq", 1, T.pl[7:8, :], T.plc[0:1, :], ["plc"], [])
    finish()
